import numpy as np
import ml_dtypes


def mxq(x, axis, fmt="e4m3"):
    dtype, down = {"e4m3": (ml_dtypes.float8_e4m3fn, 7), "e5m2": (ml_dtypes.float8_e5m2, 14)}[fmt]
    v = np.moveaxis(np.asarray(x, np.float32).astype(ml_dtypes.bfloat16).astype(np.float64), axis, -1)
    blocks = v.reshape(v.shape[:-1] + (-1, 32))
    amax = np.abs(blocks).max(-1, keepdims=True)
    byte = np.maximum(np.where(amax > 0, np.frexp(amax)[1] - 1 + 127, 0) - down, 1)
    scale = np.exp2(byte - 127.0)
    codes = (blocks / scale).astype(np.float32).astype(dtype).astype(np.float64)
    return np.moveaxis((codes * scale).reshape(v.shape), -1, axis)


WIDE = False


def mx_kscale(k):
    if not WIDE:
        return np.ones(k)
    levels = np.array([10, -10, 5, -5, 0])
    if k % 512:
        return np.exp2(np.random.permutation(np.resize(levels, k // 32))).repeat(32)
    a = np.empty((k // 512, 16))
    for p in range(k // 512):
        a[p, :8] = np.random.permutation(np.resize(levels, 8))
        for g in range(8):
            far = levels[np.abs(levels - a[p, g]) >= 10]
            a[p, g + 8] = far[np.random.randint(len(far))]
    return np.exp2(a.ravel()).repeat(32)


def f64(x):
    return np.asarray(x).astype(np.float64)


def striped(idx):
    return np.tile(idx.reshape(-1, 16).T, (8, 1)).astype(np.uint16)


def unstriped(offs):
    return offs[:16].T.reshape(-1).astype(np.int64)


E2M1 = np.array([0.0, 0.5, 1.0, 1.5, 2.0, 3.0, 4.0, 6.0, -0.0, -0.5, -1.0, -1.5, -2.0, -3.0, -4.0, -6.0])


def pack_weight(w, fmt):
    k, n = w.shape
    w = f64(np.asarray(w, np.float32).astype(ml_dtypes.bfloat16)).reshape(k // 32, 32, n)
    amax = np.abs(w).max(1)
    if fmt == "e4m3":
        byte = np.frexp(amax)[1] - 1 + 127 - 7
    else:
        mant, ex = np.frexp(amax / 6.0)
        byte = np.where(mant > 0.5, ex, ex - 1) + 127
    byte = np.clip(np.where(amax > 0, byte, 1), 1, 254)
    scaled = (w * np.exp2(127.0 - byte)[:, None, :]).reshape(k, n).astype(np.float32)
    by_word = np.ascontiguousarray(scaled.reshape(k // 512, 128, 4, n).transpose(0, 1, 3, 2))
    if fmt == "e4m3":
        words = by_word.astype(ml_dtypes.float8_e4m3fn).view(np.uint8)
    else:
        c = by_word.astype(ml_dtypes.float4_e2m1fn).view(np.uint8) & 0xF
        words = (c[..., 0::2] | (c[..., 1::2] << 4)).reshape(k // 512, 128, 2 * n)
    return np.ascontiguousarray(words), np.ascontiguousarray(byte.astype(np.uint8).reshape(k // 512, 16, n))


def unpack_weight(words, scales, fmt):
    g, _, n = scales.shape
    words = np.ascontiguousarray(words).reshape(g, 128, n, -1)
    if fmt == "e4m3":
        vals = words.view(ml_dtypes.float8_e4m3fn).astype(np.float64)
    else:
        nib = np.empty((g, 128, n, 4), np.uint8)
        nib[..., 0::2] = words & 0xF
        nib[..., 1::2] = words >> 4
        vals = E2M1[nib]
    vals = vals * np.repeat(np.exp2(scales.astype(np.float64) - 127.0), 8, axis=1)[..., None]
    return vals.transpose(0, 1, 3, 2).reshape(g * 512, n)


def pack_table(v):
    words, scales = pack_weight(v, "e4m3")
    return np.concatenate([words.reshape(words.shape[0], -1), scales.reshape(scales.shape[0], -1)], axis=1)


def unpack_table(tab):
    g, t = tab.shape[0], tab.shape[1] // 528
    return unpack_weight(tab[:, :512 * t].reshape(g, 128, t, 4), tab[:, 512 * t:].reshape(g, 16, t), "e4m3")


K, H, M, T, S = 512, 1024, 256, 4096, 1536


def setup_inputs():
    n = np.random.standard_normal
    s = mx_kscale(K)[:, None]
    u = mx_kscale(H)[:, None]
    w2 = 1.4 * n((H, M)) / np.sqrt(H) / u
    p_w8 = pack_weight(w2[:512], "e4m3")
    p_w4 = pack_weight(w2[512:], "e2m1")
    return {
        "tab": pack_table(n((K, T)) * s),
        "w1": (n((K, H)) / np.sqrt(K) / s * u.T).astype(np.float32),
        "w8_words": p_w8[0],
        "w8_scales": p_w8[1],
        "w4_words": p_w4[0],
        "w4_scales": p_w4[1],
        "b": (0.3 * n(256)).astype(np.float32),
        "offs": striped(np.random.permutation(T)[:S]),
    }


def reference(tab, w1, w8_words, w8_scales, w4_words, w4_scales, b, offs):
    tab_ = unpack_table(tab)[:, unstriped(offs)]
    w1_ = mxq(f64(w1), 0, "e4m3")
    w8_ = unpack_weight(w8_words, w8_scales, "e4m3")
    w4_ = unpack_weight(w4_words, w4_scales, "e2m1")
    h_ = mxq(np.maximum(w1_.T @ tab_, 0.0), 0, "e4m3")
    y = w8_.T @ h_[:512] + w4_.T @ h_[512:]
    return y + f64(b)[:, None]

@@ -1,0 +1,229 @@
+from contextlib import ExitStack
+
+import concourse.mybir as mybir
+
+K, H, M, T, S = 512, 1024, 256, 4096, 1536
+FLOPS = 2 * S * (K * H + H * M)
+
+F32 = mybir.dt.float32
+BF16 = mybir.dt.bfloat16
+I32 = mybir.dt.int32
+U32 = mybir.dt.uint32
+U16 = mybir.dt.uint16
+U8 = mybir.dt.uint8
+FP8X4 = mybir.dt.float8_e4m3fn_x4
+FP4X4 = mybir.dt.float4_e2m1fn_x4
+RELU = mybir.ActivationFunctionType.Relu
+IDENTITY = mybir.ActivationFunctionType.Identity
+ADD = mybir.AluOpType.add
+MULT = mybir.AluOpType.mult
+
+P = 128
+CHUNK = 512
+BLOCK = 128
+GROUP = 512
+CHUNKS = S // CHUNK
+BLOCKS = CHUNK // BLOCK
+GROUPS = H // GROUP
+PIECE = 256
+
+CONVERT = ["s","s","s","v"]
+RELU_ENGINE = [["ssss","ssss"],["sssv","ssvv"],["svsv","svsv"]]
+GROUPED_TAG = ["turn", "grouped1"]
+OUT_ENGINE = ["ss","ss","sv"]
+
+
+def tile_list_tabmlp_mix_bias_kernel(
+    tc, tab, w1, w8_words, w8_scales, w4_words, w4_scales, b, offs, out
+):
+    nc = tc.nc
+    with ExitStack() as ctx:
+        keep = ctx.enter_context(tc.tile_pool(name="keep", bufs=1))
+        hidden_psum = ctx.enter_context(tc.psum_pool(name="hidden_psum", bufs=6))
+        out_psum = ctx.enter_context(tc.psum_pool(name="out_psum", bufs=2))
+
+        offsets = keep.tile([P, S // 16], U16, name="offsets")
+        nc.sync.dma_start(offsets[:], offs)
+
+        table_words = keep.tile([P, T], I32, name="table_words", align_bytes=64)
+        words_hbm = tab[0, 0 : 512 * T].rearrange("(p c) -> p c", p=P).bitcast(I32)
+        for half in range(2):
+            cols = slice(half * T // 2, (half + 1) * T // 2)
+            nc.sync.dma_start(table_words[:, cols], words_hbm[:, cols])
+
+        table_scales = keep.tile([P, T], U8, name="table_scales", align_bytes=64)
+        nc.vector.memset(table_scales[:].bitcast(I32), 0)
+        scales_hbm = tab[0, 512 * T : 528 * T].rearrange("(q t) -> q t", q=16).bitcast(I32)
+        for quad in range(4):
+            nc.sync.dma_start(
+                table_scales[:].bitcast(I32)[32 * quad : 32 * quad + 4, :], scales_hbm[4 * quad : 4 * quad + 4, :]
+            )
+
+        w1_hbm = w1.rearrange("(p j) c -> p j c", j=4)
+        w1_raw = []
+        for piece in range(H // PIECE):
+            raw = keep.tile([P, 4, PIECE], F32, name=f"w1_raw{piece}")
+            nc.sync.dma_start(raw[:], w1_hbm[:, :, piece * PIECE : (piece + 1) * PIECE])
+            w1_raw.append(raw)
+
+        w8 = keep.tile([P, M], I32, name="w8", align_bytes=64)
+        nc.sync.dma_start(w8[:], w8_words[0].rearrange("p n i -> p (n i)").bitcast(I32))
+        w4 = keep.tile([P, 2 * M], U8, name="w4", align_bytes=64)
+        nc.sync.dma_start(w4[:].bitcast(I32), w4_words[0].bitcast(I32))
+
+        w_scales = keep.tile([P, 2, M], U8, name="w_scales", align_bytes=64)
+        nc.vector.memset(w_scales[:].rearrange("p g n -> p (g n)").bitcast(I32), 0)
+        for g, src in enumerate((w8_scales, w4_scales)):
+            for quad in range(4):
+                nc.sync.dma_start(
+                    w_scales[32 * quad : 32 * quad + 4, g, :].bitcast(I32), src[0, 4 * quad : 4 * quad + 4, :].bitcast(I32)
+                )
+        bias = keep.tile([P, 2], F32, name="bias")
+        nc.sync.dma_start(bias[:], b.rearrange("(m p) -> p m", p=P))
+
+        x_words = [None] * CHUNKS
+        x_scales = [None] * CHUNKS
+
+        def pick_tile(chunks, tag):
+            picked = keep.tile([P, 5 * CHUNK * len(chunks)], U8, name=f"picked{chunks[0]}", tag=tag, align_bytes=64)
+            words = picked[:, 0 : 4 * CHUNK * len(chunks)].bitcast(U32)
+            for i, c in enumerate(chunks):
+                x_words[c] = words[:, i * CHUNK : (i + 1) * CHUNK]
+                first = (4 * len(chunks) + i) * CHUNK
+                x_scales[c] = picked[:, first : first + CHUNK]
+
+        def gather(c):
+            listed = offsets[:, c * (CHUNK // 16) : (c + 1) * (CHUNK // 16)]
+            nc.vector.tensor_copy(x_words[c], table_words[:].bitcast(U32).indirect(listed))
+            nc.vector.tensor_copy(x_scales[c], table_scales[:].indirect(listed))
+
+        w1_codes = []
+        w1_scales = []
+
+        def prepare_w1(g):
+            grouped = keep.tile([P, 4 * GROUP], BF16, name=f"w1_grouped{g}", tag=GROUPED_TAG[g], align_bytes=64)
+            order = grouped[:].rearrange("p (t m j) -> p m j t", t=4, j=4)
+            per_group = GROUP // PIECE
+            for i in range(per_group):
+                piece = g * per_group + i
+                m = slice(i * PIECE // 4, (i + 1) * PIECE // 4)
+                dst = order[:, m, :, :]
+                src = w1_raw[piece][:].rearrange("p j (m t) -> p m j t", t=4)
+                engine = CONVERT[piece]
+                if engine == "s":
+                    nc.scalar.copy(dst, src)
+                elif engine == "g":
+                    nc.gpsimd.tensor_scalar(dst, src, 1.0, 0.0, MULT, ADD)
+                else:
+                    nc.vector.tensor_copy(dst, src)
+            codes = keep.tile([P, GROUP], U32, name=f"w1_codes{g}", align_bytes=64)
+            scales = keep.tile([P, GROUP], U8, name=f"w1_scales{g}", align_bytes=64)
+            nc.vector.quantize_mx(out=codes[:].bitcast(FP8X4), scales=scales[:], in_=grouped[:])
+            w1_codes.append(codes)
+            w1_scales.append(scales)
+
+        h_grouped = {}
+        h_codes = {}
+        h_scales = {}
+        for c in range(CHUNKS):
+            for g in range(GROUPS):
+                h_grouped[c, g] = keep.tile([P, 4 * CHUNK], BF16, name=f"h_grouped{c}{g}", align_bytes=64)
+                h_codes[c, g] = keep.tile([P, CHUNK], U32, name=f"h_codes{c}{g}", align_bytes=64)
+                h_scales[c, g] = keep.tile([P, CHUNK], U8, name=f"h_scales{c}{g}", align_bytes=64)
+
+        def hidden(c, g, block):
+            bank = hidden_psum.tile([P, 4, BLOCK], F32, name="bank")
+            cols = slice(block * BLOCK, (block + 1) * BLOCK)
+            for t in range(4):
+                rows = slice(t * P, (t + 1) * P)
+                nc.tensor.matmul_mx(
+                    out=bank[:, t, :],
+                    lhsT=w1_codes[g][:, rows].bitcast(FP8X4),
+                    lhsT_scale=w1_scales[g][:, rows],
+                    rhs=x_words[c][:, cols].bitcast(FP8X4),
+                    rhs_scale=x_scales[c][:, cols],
+                    start=True,
+                    stop=True,
+                )
+            dst = h_grouped[c, g][:, 4 * BLOCK * block : 4 * BLOCK * (block + 1)].rearrange("p (n t) -> p n t", t=4)
+            src = bank[:].rearrange("p t n -> p n t")
+            if RELU_ENGINE[c][g][block] == "s":
+                nc.scalar.activation(dst, src, RELU)
+            else:
+                nc.vector.tensor_scalar_max(dst, src, 0.0)
+
+        def quantize(c, g, block0, blocks):
+            cols = slice(block0 * BLOCK, (block0 + blocks) * BLOCK)
+            nc.vector.quantize_mx(
+                out=h_codes[c, g][:, cols].bitcast(FP8X4),
+                scales=h_scales[c, g][:, cols],
+                in_=h_grouped[c, g][:, 4 * BLOCK * block0 : 4 * BLOCK * (block0 + blocks)],
+            )
+
+        out_hbm = out.rearrange("(m p) j -> p m j", p=P)
+
+        def output(c, block0, blocks, width, engines):
+            total = blocks * BLOCK
+            stage = keep.tile([P, 2, total], F32, name=f"stage{c}_{block0}")
+            for m in range(2):
+                acc = out_psum.tile([P, CHUNK], F32, name="acc")
+                rows = slice(m * P, (m + 1) * P)
+                for n in range(0, total, width):
+                    cols = slice(block0 * BLOCK + n, block0 * BLOCK + n + width)
+                    nc.tensor.matmul_mx(
+                        out=acc[:, n : n + width],
+                        lhsT=w8[:, rows].bitcast(FP8X4),
+                        lhsT_scale=w_scales[:, 0, rows],
+                        rhs=h_codes[c, 0][:, cols].bitcast(FP8X4),
+                        rhs_scale=h_scales[c, 0][:, cols],
+                        start=True,
+                        stop=False,
+                    )
+                    nc.tensor.matmul_mx(
+                        out=acc[:, n : n + width],
+                        lhsT=w4[:, 2 * m * P : 2 * (m + 1) * P].bitcast(FP4X4),
+                        lhsT_scale=w_scales[:, 1, rows],
+                        rhs=h_codes[c, 1][:, cols].bitcast(FP8X4),
+                        rhs_scale=h_scales[c, 1][:, cols],
+                        start=False,
+                        stop=True,
+                    )
+                if engines[m] == "s":
+                    nc.scalar.activation(stage[:, m, :], acc[:, 0:total], IDENTITY, bias=bias[:, m : m + 1])
+                else:
+                    nc.vector.tensor_scalar(stage[:, m, :], acc[:, 0:total], bias[:, m : m + 1], None, ADD)
+            first = c * CHUNK + block0 * BLOCK
+            nc.sync.dma_start(out_hbm[:, :, first : first + total], stage[:])
+
+        pick_tile([0], "picked0")
+        gather(0)
+        prepare_w1(0)
+        for block in range(BLOCKS):
+            hidden(0, 0, block)
+        pick_tile([1, 2], "turn")
+        gather(1)
+        prepare_w1(1)
+        quantize(0, 0, 0, 4)
+        for block in range(BLOCKS):
+            hidden(0, 1, block)
+        gather(2)
+        for block in range(BLOCKS):
+            hidden(1, 0, block)
+        quantize(0, 1, 0, 4)
+        output(0, 0, 4, 512, OUT_ENGINE[0])
+        quantize(1, 0, 0, 4)
+        for block in range(BLOCKS):
+            hidden(1, 1, block)
+        for block in range(BLOCKS):
+            hidden(2, 0, block)
+        quantize(1, 1, 0, 4)
+        output(1, 0, 4, 512, OUT_ENGINE[1])
+        quantize(2, 0, 0, 4)
+        for block in range(BLOCKS):
+            hidden(2, 1, block)
+            if block == 1:
+                quantize(2, 1, 0, 2)
+        output(2, 0, 2, 128, OUT_ENGINE[2])
+        quantize(2, 1, 2, 1)
+        quantize(2, 1, 3, 1)
+        output(2, 2, 2, 128, OUT_ENGINE[2])

@@ -27,10 +27,10 @@ BLOCKS = CHUNK // BLOCK
 GROUPS = H // GROUP
 PIECE = 256
 
-CONVERT = ["s","s","s","v"]
-RELU_ENGINE = [["ssss","ssss"],["sssv","ssvv"],["svsv","svsv"]]
-GROUPED_TAG = ["turn", "grouped1"]
-OUT_ENGINE = ["ss","ss","sv"]
+CONVERT = ["s","s","v","v"]
+RELU_ENGINE = [["ssss","sssv"],["ssss","svsv"],["svsv","svsv"]]
+GROUPED_TAG = ["turn","grouped1"]
+OUT_ENGINE = ["ss","sv","sv"]
 
 
 def tile_list_tabmlp_mix_bias_kernel(
@@ -51,20 +51,25 @@ def tile_list_tabmlp_mix_bias_kernel(
             cols = slice(half * T // 2, (half + 1) * T // 2)
             nc.sync.dma_start(table_words[:, cols], words_hbm[:, cols])
 
+
         table_scales = keep.tile([P, T], U8, name="table_scales", align_bytes=64)
         nc.vector.memset(table_scales[:].bitcast(I32), 0)
+        w1_hbm = w1.rearrange("(p j) c -> p j c", j=4)
+        w1_raw = []
+
+        def load_w1(g):
+            for piece in range(g * GROUP // PIECE, (g + 1) * GROUP // PIECE):
+                raw = keep.tile([P, 4, PIECE], F32, name=f"w1_raw{piece}")
+                nc.sync.dma_start(raw[:], w1_hbm[:, :, piece * PIECE : (piece + 1) * PIECE])
+                w1_raw.append(raw)
+
+        load_w1(0)
         scales_hbm = tab[0, 512 * T : 528 * T].rearrange("(q t) -> q t", q=16).bitcast(I32)
         for quad in range(4):
             nc.sync.dma_start(
                 table_scales[:].bitcast(I32)[32 * quad : 32 * quad + 4, :], scales_hbm[4 * quad : 4 * quad + 4, :]
             )
-
-        w1_hbm = w1.rearrange("(p j) c -> p j c", j=4)
-        w1_raw = []
-        for piece in range(H // PIECE):
-            raw = keep.tile([P, 4, PIECE], F32, name=f"w1_raw{piece}")
-            nc.sync.dma_start(raw[:], w1_hbm[:, :, piece * PIECE : (piece + 1) * PIECE])
-            w1_raw.append(raw)
+        load_w1(1)
 
         w8 = keep.tile([P, M], I32, name="w8", align_bytes=64)
         nc.sync.dma_start(w8[:], w8_words[0].rearrange("p n i -> p (n i)").bitcast(I32))
@@ -81,21 +86,22 @@ def tile_list_tabmlp_mix_bias_kernel(
         bias = keep.tile([P, 2], F32, name="bias")
         nc.sync.dma_start(bias[:], b.rearrange("(m p) -> p m", p=P))
 
-        x_words = [None] * CHUNKS
-        x_scales = [None] * CHUNKS
+        x_words = []
+        x_scales = []
 
-        def pick_tile(chunks, tag):
-            picked = keep.tile([P, 5 * CHUNK * len(chunks)], U8, name=f"picked{chunks[0]}", tag=tag, align_bytes=64)
-            words = picked[:, 0 : 4 * CHUNK * len(chunks)].bitcast(U32)
-            for i, c in enumerate(chunks):
-                x_words[c] = words[:, i * CHUNK : (i + 1) * CHUNK]
-                first = (4 * len(chunks) + i) * CHUNK
-                x_scales[c] = picked[:, first : first + CHUNK]
+        def listed(c):
+            return offsets[:, c * (CHUNK // 16) : (c + 1) * (CHUNK // 16)]
 
-        def gather(c):
-            listed = offsets[:, c * (CHUNK // 16) : (c + 1) * (CHUNK // 16)]
-            nc.vector.tensor_copy(x_words[c], table_words[:].bitcast(U32).indirect(listed))
-            nc.vector.tensor_copy(x_scales[c], table_scales[:].indirect(listed))
+        def gather_words(c):
+            words = keep.tile([P, CHUNK], U32, name=f"x_words{c}", align_bytes=64)
+            nc.vector.tensor_copy(words[:], table_words[:].bitcast(U32).indirect(listed(c)))
+            x_words.append(words)
+
+        def gather_scales(first, count, tag):
+            scales = keep.tile([P, count, CHUNK], U8, name=f"x_scales{first}", tag=tag, align_bytes=64)
+            for i in range(count):
+                nc.vector.tensor_copy(scales[:, i, :], table_scales[:].indirect(listed(first + i)))
+                x_scales.append(scales[:, i, :])
 
         w1_codes = []
         w1_scales = []
@@ -195,28 +201,27 @@ def tile_list_tabmlp_mix_bias_kernel(
             first = c * CHUNK + block0 * BLOCK
             nc.sync.dma_start(out_hbm[:, :, first : first + total], stage[:])
 
-        pick_tile([0], "picked0")
-        gather(0)
+        for c in range(CHUNKS):
+            gather_words(c)
         prepare_w1(0)
+        gather_scales(0, 1, "x_scales0")
         for block in range(BLOCKS):
             hidden(0, 0, block)
-        pick_tile([1, 2], "turn")
-        gather(1)
+        gather_scales(1, 2, "turn")
+        for block in range(BLOCKS):
+            hidden(1, 0, block)
         prepare_w1(1)
         quantize(0, 0, 0, 4)
         for block in range(BLOCKS):
             hidden(0, 1, block)
-        gather(2)
-        for block in range(BLOCKS):
-            hidden(1, 0, block)
-        quantize(0, 1, 0, 4)
-        output(0, 0, 4, 512, OUT_ENGINE[0])
         quantize(1, 0, 0, 4)
+        quantize(0, 1, 0, 4)
         for block in range(BLOCKS):
             hidden(1, 1, block)
+        output(0, 0, 4, 512, OUT_ENGINE[0])
+        quantize(1, 1, 0, 4)
         for block in range(BLOCKS):
             hidden(2, 0, block)
-        quantize(1, 1, 0, 4)
         output(1, 0, 4, 512, OUT_ENGINE[1])
         quantize(2, 0, 0, 4)
         for block in range(BLOCKS):

@@ -29,7 +29,7 @@ PIECE = 256
 
 CONVERT = ["s","s","v","v"]
 RELU_ENGINE = [["ssss","sssv"],["ssss","svsv"],["svsv","svsv"]]
-GROUPED_TAG = ["turn","grouped1"]
+GROUPED_TAG = ["turn","turn"]
 OUT_ENGINE = ["ss","sv","sv"]
 
 
@@ -64,11 +64,9 @@ def tile_list_tabmlp_mix_bias_kernel(
                 w1_raw.append(raw)
 
         load_w1(0)
-        scales_hbm = tab[0, 512 * T : 528 * T].rearrange("(q t) -> q t", q=16).bitcast(I32)
-        for quad in range(4):
-            nc.sync.dma_start(
-                table_scales[:].bitcast(I32)[32 * quad : 32 * quad + 4, :], scales_hbm[4 * quad : 4 * quad + 4, :]
-            )
+        scales_hbm = tab[0, 512 * T : 528 * T].rearrange("(q r t) -> r q t", q=4, r=4).bitcast(I32)
+        for r in range(4):
+            nc.sync.dma_start(table_scales[r:P:32, :].bitcast(I32), scales_hbm[r])
         load_w1(1)
 
         w8 = keep.tile([P, M], I32, name="w8", align_bytes=64)
@@ -79,10 +77,9 @@ def tile_list_tabmlp_mix_bias_kernel(
         w_scales = keep.tile([P, 2, M], U8, name="w_scales", align_bytes=64)
         nc.vector.memset(w_scales[:].rearrange("p g n -> p (g n)").bitcast(I32), 0)
         for g, src in enumerate((w8_scales, w4_scales)):
-            for quad in range(4):
-                nc.sync.dma_start(
-                    w_scales[32 * quad : 32 * quad + 4, g, :].bitcast(I32), src[0, 4 * quad : 4 * quad + 4, :].bitcast(I32)
-                )
+            rows = src[0].rearrange("(q r) n -> r q n", r=4).bitcast(I32)
+            for r in range(4):
+                nc.sync.dma_start(w_scales[r:P:32, g, :].bitcast(I32), rows[r])
         bias = keep.tile([P, 2], F32, name="bias")
         nc.sync.dma_start(bias[:], b.rearrange("(m p) -> p m", p=P))
 
@@ -207,7 +204,7 @@ def tile_list_tabmlp_mix_bias_kernel(
         gather_scales(0, 1, "x_scales0")
         for block in range(BLOCKS):
             hidden(0, 0, block)
-        gather_scales(1, 2, "turn")
+        gather_scales(1, 2, "x_scales1")
         for block in range(BLOCKS):
             hidden(1, 0, block)
         prepare_w1(1)

from contextlib import ExitStack

import concourse.mybir as mybir

K, H, M, T, S = 512, 1024, 256, 4096, 1536
FLOPS = 2 * S * (K * H + H * M)

F32 = mybir.dt.float32
BF16 = mybir.dt.bfloat16
I32 = mybir.dt.int32
U32 = mybir.dt.uint32
U16 = mybir.dt.uint16
U8 = mybir.dt.uint8
FP8X4 = mybir.dt.float8_e4m3fn_x4
FP4X4 = mybir.dt.float4_e2m1fn_x4
RELU = mybir.ActivationFunctionType.Relu
IDENTITY = mybir.ActivationFunctionType.Identity
ADD = mybir.AluOpType.add
MULT = mybir.AluOpType.mult

P = 128
CHUNK = 512
BLOCK = 128
GROUP = 512
CHUNKS = S // CHUNK
BLOCKS = CHUNK // BLOCK
GROUPS = H // GROUP
PIECE = 256

CONVERT = ["s","s","v","v"]
RELU_ENGINE = [["ssss","sssv"],["ssss","svsv"],["svsv","svsv"]]
GROUPED_TAG = ["turn","turn"]
OUT_ENGINE = ["ss","sv","sv"]


def tile_list_tabmlp_mix_bias_kernel(
    tc, tab, w1, w8_words, w8_scales, w4_words, w4_scales, b, offs, out
):
    nc = tc.nc
    with ExitStack() as ctx:
        keep = ctx.enter_context(tc.tile_pool(name="keep", bufs=1))
        hidden_psum = ctx.enter_context(tc.psum_pool(name="hidden_psum", bufs=6))
        out_psum = ctx.enter_context(tc.psum_pool(name="out_psum", bufs=2))

        offsets = keep.tile([P, S // 16], U16, name="offsets")
        nc.sync.dma_start(offsets[:], offs)

        table_words = keep.tile([P, T], I32, name="table_words", align_bytes=64)
        words_hbm = tab[0, 0 : 512 * T].rearrange("(p c) -> p c", p=P).bitcast(I32)
        for half in range(2):
            cols = slice(half * T // 2, (half + 1) * T // 2)
            nc.sync.dma_start(table_words[:, cols], words_hbm[:, cols])


        table_scales = keep.tile([P, T], U8, name="table_scales", align_bytes=64)
        nc.vector.memset(table_scales[:].bitcast(I32), 0)
        w1_hbm = w1.rearrange("(p j) c -> p j c", j=4)
        w1_raw = []

        def load_w1(g):
            for piece in range(g * GROUP // PIECE, (g + 1) * GROUP // PIECE):
                raw = keep.tile([P, 4, PIECE], F32, name=f"w1_raw{piece}")
                nc.sync.dma_start(raw[:], w1_hbm[:, :, piece * PIECE : (piece + 1) * PIECE])
                w1_raw.append(raw)

        load_w1(0)
        scales_hbm = tab[0, 512 * T : 528 * T].rearrange("(q r t) -> r q t", q=4, r=4).bitcast(I32)
        for r in range(4):
            nc.sync.dma_start(table_scales[r:P:32, :].bitcast(I32), scales_hbm[r])
        load_w1(1)

        w8 = keep.tile([P, M], I32, name="w8", align_bytes=64)
        nc.sync.dma_start(w8[:], w8_words[0].rearrange("p n i -> p (n i)").bitcast(I32))
        w4 = keep.tile([P, 2 * M], U8, name="w4", align_bytes=64)
        nc.sync.dma_start(w4[:].bitcast(I32), w4_words[0].bitcast(I32))

        w_scales = keep.tile([P, 2, M], U8, name="w_scales", align_bytes=64)
        nc.vector.memset(w_scales[:].rearrange("p g n -> p (g n)").bitcast(I32), 0)
        for g, src in enumerate((w8_scales, w4_scales)):
            rows = src[0].rearrange("(q r) n -> r q n", r=4).bitcast(I32)
            for r in range(4):
                nc.sync.dma_start(w_scales[r:P:32, g, :].bitcast(I32), rows[r])
        bias = keep.tile([P, 2], F32, name="bias")
        nc.sync.dma_start(bias[:], b.rearrange("(m p) -> p m", p=P))

        x_words = []
        x_scales = []

        def listed(c):
            return offsets[:, c * (CHUNK // 16) : (c + 1) * (CHUNK // 16)]

        def gather_words(c):
            words = keep.tile([P, CHUNK], U32, name=f"x_words{c}", align_bytes=64)
            nc.vector.tensor_copy(words[:], table_words[:].bitcast(U32).indirect(listed(c)))
            x_words.append(words)

        def gather_scales(first, count, tag):
            scales = keep.tile([P, count, CHUNK], U8, name=f"x_scales{first}", tag=tag, align_bytes=64)
            for i in range(count):
                nc.vector.tensor_copy(scales[:, i, :], table_scales[:].indirect(listed(first + i)))
                x_scales.append(scales[:, i, :])

        w1_codes = []
        w1_scales = []

        def prepare_w1(g):
            grouped = keep.tile([P, 4 * GROUP], BF16, name=f"w1_grouped{g}", tag=GROUPED_TAG[g], align_bytes=64)
            order = grouped[:].rearrange("p (t m j) -> p m j t", t=4, j=4)
            per_group = GROUP // PIECE
            for i in range(per_group):
                piece = g * per_group + i
                m = slice(i * PIECE // 4, (i + 1) * PIECE // 4)
                dst = order[:, m, :, :]
                src = w1_raw[piece][:].rearrange("p j (m t) -> p m j t", t=4)
                engine = CONVERT[piece]
                if engine == "s":
                    nc.scalar.copy(dst, src)
                elif engine == "g":
                    nc.gpsimd.tensor_scalar(dst, src, 1.0, 0.0, MULT, ADD)
                else:
                    nc.vector.tensor_copy(dst, src)
            codes = keep.tile([P, GROUP], U32, name=f"w1_codes{g}", align_bytes=64)
            scales = keep.tile([P, GROUP], U8, name=f"w1_scales{g}", align_bytes=64)
            nc.vector.quantize_mx(out=codes[:].bitcast(FP8X4), scales=scales[:], in_=grouped[:])
            w1_codes.append(codes)
            w1_scales.append(scales)

        h_grouped = {}
        h_codes = {}
        h_scales = {}
        for c in range(CHUNKS):
            for g in range(GROUPS):
                h_grouped[c, g] = keep.tile([P, 4 * CHUNK], BF16, name=f"h_grouped{c}{g}", align_bytes=64)
                h_codes[c, g] = keep.tile([P, CHUNK], U32, name=f"h_codes{c}{g}", align_bytes=64)
                h_scales[c, g] = keep.tile([P, CHUNK], U8, name=f"h_scales{c}{g}", align_bytes=64)

        def hidden(c, g, block):
            bank = hidden_psum.tile([P, 4, BLOCK], F32, name="bank")
            cols = slice(block * BLOCK, (block + 1) * BLOCK)
            for t in range(4):
                rows = slice(t * P, (t + 1) * P)
                nc.tensor.matmul_mx(
                    out=bank[:, t, :],
                    lhsT=w1_codes[g][:, rows].bitcast(FP8X4),
                    lhsT_scale=w1_scales[g][:, rows],
                    rhs=x_words[c][:, cols].bitcast(FP8X4),
                    rhs_scale=x_scales[c][:, cols],
                    start=True,
                    stop=True,
                )
            dst = h_grouped[c, g][:, 4 * BLOCK * block : 4 * BLOCK * (block + 1)].rearrange("p (n t) -> p n t", t=4)
            src = bank[:].rearrange("p t n -> p n t")
            if RELU_ENGINE[c][g][block] == "s":
                nc.scalar.activation(dst, src, RELU)
            else:
                nc.vector.tensor_scalar_max(dst, src, 0.0)

        def quantize(c, g, block0, blocks):
            cols = slice(block0 * BLOCK, (block0 + blocks) * BLOCK)
            nc.vector.quantize_mx(
                out=h_codes[c, g][:, cols].bitcast(FP8X4),
                scales=h_scales[c, g][:, cols],
                in_=h_grouped[c, g][:, 4 * BLOCK * block0 : 4 * BLOCK * (block0 + blocks)],
            )

        out_hbm = out.rearrange("(m p) j -> p m j", p=P)

        def output(c, block0, blocks, width, engines):
            total = blocks * BLOCK
            stage = keep.tile([P, 2, total], F32, name=f"stage{c}_{block0}")
            for m in range(2):
                acc = out_psum.tile([P, CHUNK], F32, name="acc")
                rows = slice(m * P, (m + 1) * P)
                for n in range(0, total, width):
                    cols = slice(block0 * BLOCK + n, block0 * BLOCK + n + width)
                    nc.tensor.matmul_mx(
                        out=acc[:, n : n + width],
                        lhsT=w8[:, rows].bitcast(FP8X4),
                        lhsT_scale=w_scales[:, 0, rows],
                        rhs=h_codes[c, 0][:, cols].bitcast(FP8X4),
                        rhs_scale=h_scales[c, 0][:, cols],
                        start=True,
                        stop=False,
                    )
                    nc.tensor.matmul_mx(
                        out=acc[:, n : n + width],
                        lhsT=w4[:, 2 * m * P : 2 * (m + 1) * P].bitcast(FP4X4),
                        lhsT_scale=w_scales[:, 1, rows],
                        rhs=h_codes[c, 1][:, cols].bitcast(FP8X4),
                        rhs_scale=h_scales[c, 1][:, cols],
                        start=False,
                        stop=True,
                    )
                if engines[m] == "s":
                    nc.scalar.activation(stage[:, m, :], acc[:, 0:total], IDENTITY, bias=bias[:, m : m + 1])
                else:
                    nc.vector.tensor_scalar(stage[:, m, :], acc[:, 0:total], bias[:, m : m + 1], None, ADD)
            first = c * CHUNK + block0 * BLOCK
            nc.sync.dma_start(out_hbm[:, :, first : first + total], stage[:])

        for c in range(CHUNKS):
            gather_words(c)
        prepare_w1(0)
        gather_scales(0, 1, "x_scales0")
        for block in range(BLOCKS):
            hidden(0, 0, block)
        gather_scales(1, 2, "x_scales1")
        for block in range(BLOCKS):
            hidden(1, 0, block)
        prepare_w1(1)
        quantize(0, 0, 0, 4)
        for block in range(BLOCKS):
            hidden(0, 1, block)
        quantize(1, 0, 0, 4)
        quantize(0, 1, 0, 4)
        for block in range(BLOCKS):
            hidden(1, 1, block)
        output(0, 0, 4, 512, OUT_ENGINE[0])
        quantize(1, 1, 0, 4)
        for block in range(BLOCKS):
            hidden(2, 0, block)
        output(1, 0, 4, 512, OUT_ENGINE[1])
        quantize(2, 0, 0, 4)
        for block in range(BLOCKS):
            hidden(2, 1, block)
            if block == 1:
                quantize(2, 1, 0, 2)
        output(2, 0, 2, 128, OUT_ENGINE[2])
        quantize(2, 1, 2, 1)
        quantize(2, 1, 3, 1)
        output(2, 2, 2, 128, OUT_ENGINE[2])
